import numpy as np
import ml_dtypes


def mxq(x, axis, fmt="e4m3"):
    dtype, down = {"e4m3": (ml_dtypes.float8_e4m3fn, 7), "e5m2": (ml_dtypes.float8_e5m2, 14)}[fmt]
    v = np.moveaxis(np.asarray(x, np.float32).astype(ml_dtypes.bfloat16).astype(np.float64), axis, -1)
    blocks = v.reshape(v.shape[:-1] + (-1, 32))
    amax = np.abs(blocks).max(-1, keepdims=True)
    byte = np.maximum(np.where(amax > 0, np.frexp(amax)[1] - 1 + 127, 0) - down, 1)
    scale = np.exp2(byte - 127.0)
    codes = (blocks / scale).astype(np.float32).astype(dtype).astype(np.float64)
    return np.moveaxis((codes * scale).reshape(v.shape), -1, axis)


WIDE = False


def mx_kscale(k):
    if not WIDE:
        return np.ones(k)
    levels = np.array([30, -30])
    if k % 512:
        return np.exp2(np.random.permutation(np.resize(levels, k // 32))).repeat(32)
    a = np.empty((k // 512, 16))
    for p in range(k // 512):
        a[p, :8] = np.random.permutation(np.resize(levels, 8))
        for g in range(8):
            far = levels[np.abs(levels - a[p, g]) >= 10]
            a[p, g + 8] = far[np.random.randint(len(far))]
    return np.exp2(a.ravel()).repeat(32)


def f64(x):
    return np.asarray(x).astype(np.float64)


def striped(idx):
    return np.tile(np.asarray(idx).reshape(-1, 16).T, (8, 1)).astype(np.uint16)


def unstriped(offs):
    return offs[:16].T.reshape(-1).astype(np.int64)


E2M1 = np.array([0.0, 0.5, 1.0, 1.5, 2.0, 3.0, 4.0, 6.0, -0.0, -0.5, -1.0, -1.5, -2.0, -3.0, -4.0, -6.0])


def pack_weight(w, fmt):
    k, n = w.shape
    w = f64(np.asarray(w, np.float32).astype(ml_dtypes.bfloat16)).reshape(k // 32, 32, n)
    amax = np.abs(w).max(1)
    if fmt in ("e4m3", "e5m2"):
        byte = np.frexp(amax)[1] - 1 + 127 - (7 if fmt == "e4m3" else 14)
    else:
        mant, ex = np.frexp(amax / 6.0)
        byte = np.where(mant > 0.5, ex, ex - 1) + 127
    byte = np.clip(np.where(amax > 0, byte, 1), 1, 254)
    scaled = (w * np.exp2(127.0 - byte)[:, None, :]).reshape(k, n).astype(np.float32)
    by_word = np.ascontiguousarray(scaled.reshape(k // 512, 128, 4, n).transpose(0, 1, 3, 2))
    if fmt in ("e4m3", "e5m2"):
        words = by_word.astype(ml_dtypes.float8_e4m3fn if fmt == "e4m3" else ml_dtypes.float8_e5m2).view(np.uint8)
    else:
        c = by_word.astype(ml_dtypes.float4_e2m1fn).view(np.uint8) & 0xF
        words = (c[..., 0::2] | (c[..., 1::2] << 4)).reshape(k // 512, 128, 2 * n)
    return np.ascontiguousarray(words), np.ascontiguousarray(byte.astype(np.uint8).reshape(k // 512, 16, n))


def unpack_weight(words, scales, fmt):
    g, _, n = scales.shape
    words = np.ascontiguousarray(words).reshape(g, 128, n, -1)
    if fmt in ("e4m3", "e5m2"):
        vals = words.view(ml_dtypes.float8_e4m3fn if fmt == "e4m3" else ml_dtypes.float8_e5m2).astype(np.float64)
    else:
        nib = np.empty((g, 128, n, 4), np.uint8)
        nib[..., 0::2] = words & 0xF
        nib[..., 1::2] = words >> 4
        vals = E2M1[nib]
    vals = vals * np.repeat(np.exp2(scales.astype(np.float64) - 127.0), 8, axis=1)[..., None]
    return vals.transpose(0, 1, 3, 2).reshape(g * 512, n)


K, T, J, N = 1024, 1024, 256, 256


def setup_inputs():
    n = np.random.standard_normal
    idx = np.random.permutation(T)[:J]
    idx2 = np.random.permutation(T)[:J]
    fk = mx_kscale(K)
    xtp = pack_weight(n((K, T)) * np.random.uniform(0.4, 1.6, (1, T)) / fk[:, None], "e4m3")
    wap = pack_weight(n((K, N)) * 1 / np.sqrt(K) * fk[:, None], "e5m2")
    return {
        "xt_words": xtp[0],
        "xt_scales": xtp[1],
        "wa_words": wap[0],
        "wa_scales": wap[1],
        "wb": (n((K, N)) * 1 / np.sqrt(K) * fk[:, None]).astype(np.float32),
        "bi": (np.random.uniform(-0.6, 0.6, (1, N))).astype(np.float32),
        "offs": striped(idx),
        "offs2": striped(idx2),
    }


def reference(xt_words, xt_scales, wa_words, wa_scales, wb, bi, offs, offs2):
    idx = unstriped(offs)
    idx2 = unstriped(offs2)
    xtu = unpack_weight(xt_words, xt_scales, "e4m3")
    wau = unpack_weight(wa_words, wa_scales, "e5m2")
    xtidxg = xtu[:, idx]
    a = xtidxg.T @ wau
    xtidx2g = xtu[:, idx2]
    wbq = mxq(f64(wb), 0, "e5m2")
    b0 = xtidx2g.T @ wbq
    b2 = b0 + f64(bi)
    ea = np.mean(np.square(a), axis=1, keepdims=True)
    eb = np.mean(np.square(b2), axis=1, keepdims=True)
    y = (a - b2) * (ea - eb)
    return y

@@ -1,0 +1,138 @@
+from contextlib import ExitStack
+
+import concourse.mybir as mybir
+from concourse.masks import make_identity
+
+K, T, J, N = 1024, 1024, 256, 256
+FLOPS = 2 * 2 * K * J * N
+
+F32 = mybir.dt.float32
+BF16 = mybir.dt.bfloat16
+I32 = mybir.dt.int32
+U32 = mybir.dt.uint32
+U16 = mybir.dt.uint16
+U8 = mybir.dt.uint8
+E4M3 = mybir.dt.float8_e4m3fn_x4
+E5M2 = mybir.dt.float8_e5m2_x4
+ALU = mybir.AluOpType
+ACT = mybir.ActivationFunctionType
+
+P = 128
+PACK = 4
+PASSES = K // (P * PACK)
+QUADS = 4
+JT = J // P
+
+
+def tile_list_rows_twotokens_energygap_kernel(tc, xt_words, xt_scales, wa_words, wa_scales, wb, bi, offs, offs2, out):
+    nc = tc.nc
+    with ExitStack() as ctx:
+        sb = ctx.enter_context(tc.tile_pool(name="sb", bufs=1))
+        ps = ctx.enter_context(tc.psum_pool(name="ps", bufs=1))
+
+        list_a = sb.tile([P, J // 16], U16, name="list_a")
+        list_b = sb.tile([P, J // 16], U16, name="list_b")
+        x_planes = sb.tile([P, PASSES * T], U8, name="x_planes", align_bytes=64)
+        wa_planes = sb.tile([P, PASSES * N], U8, name="wa_planes", align_bytes=64)
+        x_words = [sb.tile([P, T], U32, name=f"x_words{z}", align_bytes=64) for z in range(PASSES)]
+        wa_codes = [sb.tile([P, N], U32, name=f"wa_codes{z}", align_bytes=64) for z in range(PASSES)]
+        wb_raw = [sb.tile([P, PACK, N], F32, name=f"wb_raw{z}") for z in range(PASSES)]
+        bias_col = sb.tile([P, 2], F32, name="bias_col")
+
+        nc.vector.memset(x_planes[:].bitcast(I32), 0)
+        nc.gpsimd.memset(wa_planes[:].bitcast(I32), 0)
+
+        def load_words(dst, src):
+            nc.sync.dma_start(out=dst[:].bitcast(I32), in_=src.rearrange("p c r -> p (c r)").bitcast(I32))
+
+        def load_planes(queue, dst, src):
+            for q in range(QUADS):
+                queue.dma_start(
+                    out=dst[32 * q : 32 * q + 4, :].bitcast(I32).rearrange("p (z c) -> p z c", z=PASSES),
+                    in_=src[:, 4 * q : 4 * q + 4, :].rearrange("z r c -> r z c").bitcast(I32),
+                )
+
+        def load_wb(z):
+            nc.sync.dma_start(out=wb_raw[z][:], in_=wb[512 * z : 512 * (z + 1), :].rearrange("(p t) n -> p t n", t=PACK))
+
+        nc.sync.dma_start(list_a[:], offs)
+        nc.sync.dma_start(list_b[:], offs2)
+        load_words(x_words[0], xt_words[0])
+        load_planes(nc.scalar, x_planes, xt_scales)
+        load_wb(0)
+        load_words(wa_codes[0], wa_words[0])
+        load_wb(1)
+        load_words(x_words[1], xt_words[1])
+        load_words(wa_codes[1], wa_words[1])
+        nc.gpsimd.dma_start(out=bias_col[:], in_=bi.rearrange("o (p c) -> p (o c)", c=2))
+        load_planes(nc.gpsimd, wa_planes, wa_scales)
+
+        ident = sb.tile([P, P], F32, name="ident")
+        make_identity(nc, ident[:])
+        bias_ps = ps.tile([P, 2, P], F32, name="bias_ps")
+        for c in range(2):
+            nc.tensor.transpose(bias_ps[:, c, :], bias_col[:, c : c + 1].to_broadcast([P, P]), ident[:])
+        bias = sb.tile([P, N], F32, name="bias")
+        nc.scalar.copy(out=bias[:].rearrange("q (p c) -> q p c", c=2), in_=bias_ps[:].rearrange("q c p -> q p c"))
+
+        lists = (list_a, list_b)
+        g_words = [[sb.tile([P, J], U32, name=f"g_words{l}{z}", align_bytes=64) for z in range(PASSES)] for l in range(2)]
+        g_planes = [[sb.tile([P, J], U8, name=f"g_planes{l}{z}", align_bytes=64) for z in range(PASSES)] for l in range(2)]
+        wb_bf = [sb.tile([P, N, PACK], BF16, name=f"wb_bf{z}", align_bytes=64) for z in range(PASSES)]
+        wb_codes = [sb.tile([P, N], U32, name=f"wb_codes{z}", align_bytes=64) for z in range(PASSES)]
+        wb_planes = [sb.tile([P, N], U8, name=f"wb_planes{z}", align_bytes=64) for z in range(PASSES)]
+
+        def gather_words(l, z, cols):
+            nc.vector.tensor_copy(g_words[l][z][:, cols], x_words[z][:].indirect(lists[l][:, cols.start // 16 : cols.stop // 16]))
+
+        for l in range(2):
+            gather_words(l, 0, slice(0, J))
+        for z in range(PASSES):
+            for l in range(2):
+                nc.vector.tensor_copy(g_planes[l][z][:], x_planes[:, z * T : (z + 1) * T].indirect(lists[l][:]))
+        for z in range(PASSES):
+            nc.scalar.copy(out=wb_bf[z][:], in_=wb_raw[z][:].rearrange("p t n -> p n t"))
+            nc.vector.quantize_mx(out=wb_codes[z][:].bitcast(E5M2), scales=wb_planes[z][:], in_=wb_bf[z][:].rearrange("p n t -> p (n t)"))
+
+        acc = [[ps.tile([P, N], F32, name=f"acc{l}{j}") for j in range(JT)] for l in range(2)]
+        w_codes = (wa_codes, wb_codes)
+        w_planes = ([wa_planes[:, z * N : (z + 1) * N] for z in range(PASSES)], [wb_planes[z][:] for z in range(PASSES)])
+
+        def product(l, j, z):
+            cols = slice(j * P, (j + 1) * P)
+            nc.tensor.matmul_mx(
+                out=acc[l][j][:],
+                lhsT=g_words[l][z][:, cols].bitcast(E4M3),
+                lhsT_scale=g_planes[l][z][:, cols],
+                rhs=w_codes[l][z][:].bitcast(E5M2),
+                rhs_scale=w_planes[l][z],
+                start=(z == 0),
+                stop=(z == PASSES - 1),
+            )
+
+        for j in range(JT):
+            for l in (0, 1):
+                product(l, j, 0)
+        for j in range(JT):
+            for l in (1, 0):
+                gather_words(l, 1, slice(j * P, (j + 1) * P))
+                product(l, j, 1)
+
+        root = 1.0 / 16.0
+        b2 = [sb.tile([P, N], F32, name=f"b2{j}") for j in range(JT)]
+        gap = [sb.tile([P, N], F32, name=f"gap{j}") for j in range(JT)]
+        sq = [sb.tile([P, N], F32, name=f"sq{j}") for j in range(2 * JT)]
+        ea = [sb.tile([P, 1], F32, name=f"ea{j}") for j in range(JT)]
+        eb = [sb.tile([P, 1], F32, name=f"eb{j}") for j in range(JT)]
+        de = [sb.tile([P, 1], F32, name=f"de{j}") for j in range(JT)]
+        res = [sb.tile([P, N], F32, name=f"res{j}") for j in range(JT)]
+        for j in range(JT):
+            nc.scalar.activation(out=sq[2 * j][:], in_=acc[0][j][:], func=ACT.Square, scale=root, accum_out=ea[j][:])
+            nc.vector.tensor_tensor(b2[j][:], acc[1][j][:], bias[:], ALU.add)
+        for j in range(JT):
+            nc.scalar.activation(out=sq[2 * j + 1][:], in_=b2[j][:], func=ACT.Square, scale=root, accum_out=eb[j][:])
+            nc.vector.tensor_tensor(gap[j][:], acc[0][j][:], b2[j][:], ALU.subtract)
+        for j in range(JT):
+            nc.vector.tensor_tensor(de[j][:], ea[j][:], eb[j][:], ALU.subtract)
+            nc.vector.tensor_scalar(res[j][:], gap[j][:], de[j][:], None, ALU.mult)
+            (nc.sync, nc.scalar)[j].dma_start(out=out[j * P : (j + 1) * P, :], in_=res[j][:])

@@ -32,15 +32,17 @@ def tile_list_rows_twotokens_energygap_kernel(tc, xt_words, xt_scales, wa_words,
 
         list_a = sb.tile([P, J // 16], U16, name="list_a")
         list_b = sb.tile([P, J // 16], U16, name="list_b")
-        x_planes = sb.tile([P, PASSES * T], U8, name="x_planes", align_bytes=64)
+        x_planes = sb.tile([P, T], U8, name="x_planes", align_bytes=64)
         wa_planes = sb.tile([P, PASSES * N], U8, name="wa_planes", align_bytes=64)
         x_words = [sb.tile([P, T], U32, name=f"x_words{z}", align_bytes=64) for z in range(PASSES)]
-        wa_codes = [sb.tile([P, N], U32, name=f"wa_codes{z}", align_bytes=64) for z in range(PASSES)]
+        wa_all = sb.tile([P, PASSES, N], U32, name="wa_all", align_bytes=64)
+        moved = sb.tile([P, 2, J], U8, name="moved", align_bytes=64)
         wb_raw = [sb.tile([P, PACK, N], F32, name=f"wb_raw{z}") for z in range(PASSES)]
         bias_col = sb.tile([P, 2], F32, name="bias_col")
 
         nc.vector.memset(x_planes[:].bitcast(I32), 0)
-        nc.gpsimd.memset(wa_planes[:].bitcast(I32), 0)
+        nc.vector.memset(wa_planes[:].bitcast(I32), 0)
+        nc.vector.memset(moved[:].bitcast(I32), 0)
 
         def load_words(dst, src):
             nc.sync.dma_start(out=dst[:].bitcast(I32), in_=src.rearrange("p c r -> p (c r)").bitcast(I32))
@@ -56,28 +58,23 @@ def tile_list_rows_twotokens_energygap_kernel(tc, xt_words, xt_scales, wa_words,
             nc.sync.dma_start(out=wb_raw[z][:], in_=wb[512 * z : 512 * (z + 1), :].rearrange("(p t) n -> p t n", t=PACK))
 
         nc.sync.dma_start(list_a[:], offs)
-        nc.sync.dma_start(list_b[:], offs2)
-        load_words(x_words[0], xt_words[0])
-        load_planes(nc.scalar, x_planes, xt_scales)
         load_wb(0)
-        load_words(wa_codes[0], wa_words[0])
-        load_wb(1)
+        nc.sync.dma_start(list_b[:], offs2)
+        for q in range(QUADS):
+            nc.sync.dma_start(out=x_planes[32 * q : 32 * q + 8, :].bitcast(I32), in_=xt_scales[:, 4 * q : 4 * q + 4, :].bitcast(I32))
+        load_words(x_words[0], xt_words[0])
         load_words(x_words[1], xt_words[1])
-        load_words(wa_codes[1], wa_words[1])
+        nc.sync.dma_start(out=wa_all[:].bitcast(I32), in_=wa_words.rearrange("z p c r -> p z (c r)").bitcast(I32))
+        load_planes(nc.sync, wa_planes, wa_scales)
+        load_wb(1)
         nc.gpsimd.dma_start(out=bias_col[:], in_=bi.rearrange("o (p c) -> p (o c)", c=2))
-        load_planes(nc.gpsimd, wa_planes, wa_scales)
 
         ident = sb.tile([P, P], F32, name="ident")
         make_identity(nc, ident[:])
-        bias_ps = ps.tile([P, 2, P], F32, name="bias_ps")
-        for c in range(2):
-            nc.tensor.transpose(bias_ps[:, c, :], bias_col[:, c : c + 1].to_broadcast([P, P]), ident[:])
-        bias = sb.tile([P, N], F32, name="bias")
-        nc.scalar.copy(out=bias[:].rearrange("q (p c) -> q p c", c=2), in_=bias_ps[:].rearrange("q c p -> q p c"))
 
         lists = (list_a, list_b)
         g_words = [[sb.tile([P, J], U32, name=f"g_words{l}{z}", align_bytes=64) for z in range(PASSES)] for l in range(2)]
-        g_planes = [[sb.tile([P, J], U8, name=f"g_planes{l}{z}", align_bytes=64) for z in range(PASSES)] for l in range(2)]
+        g_planes = sb.tile([P, 2, J], U8, name="g_planes", align_bytes=64)
         wb_bf = [sb.tile([P, N, PACK], BF16, name=f"wb_bf{z}", align_bytes=64) for z in range(PASSES)]
         wb_codes = [sb.tile([P, N], U32, name=f"wb_codes{z}", align_bytes=64) for z in range(PASSES)]
         wb_planes = [sb.tile([P, N], U8, name=f"wb_planes{z}", align_bytes=64) for z in range(PASSES)]
@@ -85,17 +82,36 @@ def tile_list_rows_twotokens_energygap_kernel(tc, xt_words, xt_scales, wa_words,
         def gather_words(l, z, cols):
             nc.vector.tensor_copy(g_words[l][z][:, cols], x_words[z][:].indirect(lists[l][:, cols.start // 16 : cols.stop // 16]))
 
-        for l in range(2):
-            gather_words(l, 0, slice(0, J))
-        for z in range(PASSES):
-            for l in range(2):
-                nc.vector.tensor_copy(g_planes[l][z][:], x_planes[:, z * T : (z + 1) * T].indirect(lists[l][:]))
-        for z in range(PASSES):
-            nc.scalar.copy(out=wb_bf[z][:], in_=wb_raw[z][:].rearrange("p t n -> p n t"))
+        def round_wb(copy, z, cols):
+            copy(
+                out=wb_bf[z][:, cols, :].rearrange("p (c i) t -> p c t i", i=4),
+                in_=wb_raw[z][:, :, cols].rearrange("p t (c i) -> p c t i", i=4),
+            )
+
+        def quantize_wb(z):
             nc.vector.quantize_mx(out=wb_codes[z][:].bitcast(E5M2), scales=wb_planes[z][:], in_=wb_bf[z][:].rearrange("p n t -> p (n t)"))
 
+        for l in range(2):
+            nc.vector.tensor_copy(g_planes[:, l, :], x_planes[:].indirect(lists[l][:]))
+        nc.sync.dma_start(out=moved[0:112].bitcast(I32), in_=g_planes[4:116].bitcast(I32))
+        round_wb(nc.scalar.copy, 0, slice(0, N))
+        bias_ps = ps.tile([P, 2, P], F32, name="bias_ps")
+        for c in range(2):
+            nc.tensor.transpose(bias_ps[:, c, :], bias_col[:, c : c + 1].to_broadcast([P, P]), ident[:])
+        bias = sb.tile([P, N], F32, name="bias")
+        nc.scalar.copy(out=bias[:].rearrange("q (p c) -> q p c", c=2), in_=bias_ps[:].rearrange("q c p -> q p c"))
+
+        quantize_wb(0)
+        for l in (1, 0):
+            gather_words(l, 0, slice(0, J))
+        for l in range(2):
+            gather_words(l, 1, slice(0, J))
+        round_wb(nc.scalar.copy, 1, slice(0, N // 2))
+        round_wb(nc.vector.tensor_copy, 1, slice(N // 2, N))
+        quantize_wb(1)
+
         acc = [[ps.tile([P, N], F32, name=f"acc{l}{j}") for j in range(JT)] for l in range(2)]
-        w_codes = (wa_codes, wb_codes)
+        w_codes = ([wa_all[:, z, :] for z in range(PASSES)], [wb_codes[z][:] for z in range(PASSES)])
         w_planes = ([wa_planes[:, z * N : (z + 1) * N] for z in range(PASSES)], [wb_planes[z][:] for z in range(PASSES)])
 
         def product(l, j, z):
@@ -103,20 +119,16 @@ def tile_list_rows_twotokens_energygap_kernel(tc, xt_words, xt_scales, wa_words,
             nc.tensor.matmul_mx(
                 out=acc[l][j][:],
                 lhsT=g_words[l][z][:, cols].bitcast(E4M3),
-                lhsT_scale=g_planes[l][z][:, cols],
-                rhs=w_codes[l][z][:].bitcast(E5M2),
+                lhsT_scale=(g_planes, moved)[z][:, l, cols],
+                rhs=w_codes[l][z].bitcast(E5M2),
                 rhs_scale=w_planes[l][z],
                 start=(z == 0),
                 stop=(z == PASSES - 1),
             )
 
-        for j in range(JT):
-            for l in (0, 1):
-                product(l, j, 0)
-        for j in range(JT):
-            for l in (1, 0):
-                gather_words(l, 1, slice(j * P, (j + 1) * P))
-                product(l, j, 1)
+        for l, z in ((1, 0), (0, 0), (0, 1), (1, 1)):
+            for j in range(JT):
+                product(l, j, z)
 
         root = 1.0 / 16.0
         b2 = [sb.tile([P, N], F32, name=f"b2{j}") for j in range(JT)]
@@ -131,8 +143,8 @@ def tile_list_rows_twotokens_energygap_kernel(tc, xt_words, xt_scales, wa_words,
             nc.vector.tensor_tensor(b2[j][:], acc[1][j][:], bias[:], ALU.add)
         for j in range(JT):
             nc.scalar.activation(out=sq[2 * j + 1][:], in_=b2[j][:], func=ACT.Square, scale=root, accum_out=eb[j][:])
+            nc.scalar.activation(out=de[j][:], in_=eb[j][:], func=ACT.Identity, scale=-1.0, bias=ea[j][:])
             nc.vector.tensor_tensor(gap[j][:], acc[0][j][:], b2[j][:], ALU.subtract)
-        for j in range(JT):
-            nc.vector.tensor_tensor(de[j][:], ea[j][:], eb[j][:], ALU.subtract)
+        for j, queue in enumerate((nc.scalar, nc.sync)):
             nc.vector.tensor_scalar(res[j][:], gap[j][:], de[j][:], None, ALU.mult)
-            (nc.sync, nc.scalar)[j].dma_start(out=out[j * P : (j + 1) * P, :], in_=res[j][:])
+            queue.dma_start(out=out[j * P : (j + 1) * P, :], in_=res[j][:])

@@ -58,10 +58,10 @@ def tile_list_rows_twotokens_energygap_kernel(tc, xt_words, xt_scales, wa_words,
             nc.sync.dma_start(out=wb_raw[z][:], in_=wb[512 * z : 512 * (z + 1), :].rearrange("(p t) n -> p t n", t=PACK))
 
         nc.sync.dma_start(list_a[:], offs)
-        load_wb(0)
         nc.sync.dma_start(list_b[:], offs2)
-        for q in range(QUADS):
-            nc.sync.dma_start(out=x_planes[32 * q : 32 * q + 8, :].bitcast(I32), in_=xt_scales[:, 4 * q : 4 * q + 4, :].bitcast(I32))
+        load_wb(0)
+        for r in range(4):
+            nc.sync.dma_start(out=x_planes[r:P:16, :].bitcast(I32), in_=xt_scales[:, r:16:4, :].rearrange("z q c -> q z c").bitcast(I32))
         load_words(x_words[0], xt_words[0])
         load_words(x_words[1], xt_words[1])
         nc.sync.dma_start(out=wa_all[:].bitcast(I32), in_=wa_words.rearrange("z p c r -> p z (c r)").bitcast(I32))
@@ -93,7 +93,7 @@ def tile_list_rows_twotokens_energygap_kernel(tc, xt_words, xt_scales, wa_words,
 
         for l in range(2):
             nc.vector.tensor_copy(g_planes[:, l, :], x_planes[:].indirect(lists[l][:]))
-        nc.sync.dma_start(out=moved[0:112].bitcast(I32), in_=g_planes[4:116].bitcast(I32))
+        nc.sync.dma_start(out=moved[0:112].bitcast(I32), in_=g_planes[16:P].bitcast(I32))
         round_wb(nc.scalar.copy, 0, slice(0, N))
         bias_ps = ps.tile([P, 2, P], F32, name="bias_ps")
         for c in range(2):

from contextlib import ExitStack

import concourse.mybir as mybir
from concourse.masks import make_identity

K, T, J, N = 1024, 1024, 256, 256
FLOPS = 2 * 2 * K * J * N

F32 = mybir.dt.float32
BF16 = mybir.dt.bfloat16
I32 = mybir.dt.int32
U32 = mybir.dt.uint32
U16 = mybir.dt.uint16
U8 = mybir.dt.uint8
E4M3 = mybir.dt.float8_e4m3fn_x4
E5M2 = mybir.dt.float8_e5m2_x4
ALU = mybir.AluOpType
ACT = mybir.ActivationFunctionType

P = 128
PACK = 4
PASSES = K // (P * PACK)
QUADS = 4
JT = J // P


def tile_list_rows_twotokens_energygap_kernel(tc, xt_words, xt_scales, wa_words, wa_scales, wb, bi, offs, offs2, out):
    nc = tc.nc
    with ExitStack() as ctx:
        sb = ctx.enter_context(tc.tile_pool(name="sb", bufs=1))
        ps = ctx.enter_context(tc.psum_pool(name="ps", bufs=1))

        list_a = sb.tile([P, J // 16], U16, name="list_a")
        list_b = sb.tile([P, J // 16], U16, name="list_b")
        x_planes = sb.tile([P, T], U8, name="x_planes", align_bytes=64)
        wa_planes = sb.tile([P, PASSES * N], U8, name="wa_planes", align_bytes=64)
        x_words = [sb.tile([P, T], U32, name=f"x_words{z}", align_bytes=64) for z in range(PASSES)]
        wa_all = sb.tile([P, PASSES, N], U32, name="wa_all", align_bytes=64)
        moved = sb.tile([P, 2, J], U8, name="moved", align_bytes=64)
        wb_raw = [sb.tile([P, PACK, N], F32, name=f"wb_raw{z}") for z in range(PASSES)]
        bias_col = sb.tile([P, 2], F32, name="bias_col")

        nc.vector.memset(x_planes[:].bitcast(I32), 0)
        nc.vector.memset(wa_planes[:].bitcast(I32), 0)
        nc.vector.memset(moved[:].bitcast(I32), 0)

        def load_words(dst, src):
            nc.sync.dma_start(out=dst[:].bitcast(I32), in_=src.rearrange("p c r -> p (c r)").bitcast(I32))

        def load_planes(queue, dst, src):
            for q in range(QUADS):
                queue.dma_start(
                    out=dst[32 * q : 32 * q + 4, :].bitcast(I32).rearrange("p (z c) -> p z c", z=PASSES),
                    in_=src[:, 4 * q : 4 * q + 4, :].rearrange("z r c -> r z c").bitcast(I32),
                )

        def load_wb(z):
            nc.sync.dma_start(out=wb_raw[z][:], in_=wb[512 * z : 512 * (z + 1), :].rearrange("(p t) n -> p t n", t=PACK))

        nc.sync.dma_start(list_a[:], offs)
        nc.sync.dma_start(list_b[:], offs2)
        load_wb(0)
        for r in range(4):
            nc.sync.dma_start(out=x_planes[r:P:16, :].bitcast(I32), in_=xt_scales[:, r:16:4, :].rearrange("z q c -> q z c").bitcast(I32))
        load_words(x_words[0], xt_words[0])
        load_words(x_words[1], xt_words[1])
        nc.sync.dma_start(out=wa_all[:].bitcast(I32), in_=wa_words.rearrange("z p c r -> p z (c r)").bitcast(I32))
        load_planes(nc.sync, wa_planes, wa_scales)
        load_wb(1)
        nc.gpsimd.dma_start(out=bias_col[:], in_=bi.rearrange("o (p c) -> p (o c)", c=2))

        ident = sb.tile([P, P], F32, name="ident")
        make_identity(nc, ident[:])

        lists = (list_a, list_b)
        g_words = [[sb.tile([P, J], U32, name=f"g_words{l}{z}", align_bytes=64) for z in range(PASSES)] for l in range(2)]
        g_planes = sb.tile([P, 2, J], U8, name="g_planes", align_bytes=64)
        wb_bf = [sb.tile([P, N, PACK], BF16, name=f"wb_bf{z}", align_bytes=64) for z in range(PASSES)]
        wb_codes = [sb.tile([P, N], U32, name=f"wb_codes{z}", align_bytes=64) for z in range(PASSES)]
        wb_planes = [sb.tile([P, N], U8, name=f"wb_planes{z}", align_bytes=64) for z in range(PASSES)]

        def gather_words(l, z, cols):
            nc.vector.tensor_copy(g_words[l][z][:, cols], x_words[z][:].indirect(lists[l][:, cols.start // 16 : cols.stop // 16]))

        def round_wb(copy, z, cols):
            copy(
                out=wb_bf[z][:, cols, :].rearrange("p (c i) t -> p c t i", i=4),
                in_=wb_raw[z][:, :, cols].rearrange("p t (c i) -> p c t i", i=4),
            )

        def quantize_wb(z):
            nc.vector.quantize_mx(out=wb_codes[z][:].bitcast(E5M2), scales=wb_planes[z][:], in_=wb_bf[z][:].rearrange("p n t -> p (n t)"))

        for l in range(2):
            nc.vector.tensor_copy(g_planes[:, l, :], x_planes[:].indirect(lists[l][:]))
        nc.sync.dma_start(out=moved[0:112].bitcast(I32), in_=g_planes[16:P].bitcast(I32))
        round_wb(nc.scalar.copy, 0, slice(0, N))
        bias_ps = ps.tile([P, 2, P], F32, name="bias_ps")
        for c in range(2):
            nc.tensor.transpose(bias_ps[:, c, :], bias_col[:, c : c + 1].to_broadcast([P, P]), ident[:])
        bias = sb.tile([P, N], F32, name="bias")
        nc.scalar.copy(out=bias[:].rearrange("q (p c) -> q p c", c=2), in_=bias_ps[:].rearrange("q c p -> q p c"))

        quantize_wb(0)
        for l in (1, 0):
            gather_words(l, 0, slice(0, J))
        for l in range(2):
            gather_words(l, 1, slice(0, J))
        round_wb(nc.scalar.copy, 1, slice(0, N // 2))
        round_wb(nc.vector.tensor_copy, 1, slice(N // 2, N))
        quantize_wb(1)

        acc = [[ps.tile([P, N], F32, name=f"acc{l}{j}") for j in range(JT)] for l in range(2)]
        w_codes = ([wa_all[:, z, :] for z in range(PASSES)], [wb_codes[z][:] for z in range(PASSES)])
        w_planes = ([wa_planes[:, z * N : (z + 1) * N] for z in range(PASSES)], [wb_planes[z][:] for z in range(PASSES)])

        def product(l, j, z):
            cols = slice(j * P, (j + 1) * P)
            nc.tensor.matmul_mx(
                out=acc[l][j][:],
                lhsT=g_words[l][z][:, cols].bitcast(E4M3),
                lhsT_scale=(g_planes, moved)[z][:, l, cols],
                rhs=w_codes[l][z].bitcast(E5M2),
                rhs_scale=w_planes[l][z],
                start=(z == 0),
                stop=(z == PASSES - 1),
            )

        for l, z in ((1, 0), (0, 0), (0, 1), (1, 1)):
            for j in range(JT):
                product(l, j, z)

        root = 1.0 / 16.0
        b2 = [sb.tile([P, N], F32, name=f"b2{j}") for j in range(JT)]
        gap = [sb.tile([P, N], F32, name=f"gap{j}") for j in range(JT)]
        sq = [sb.tile([P, N], F32, name=f"sq{j}") for j in range(2 * JT)]
        ea = [sb.tile([P, 1], F32, name=f"ea{j}") for j in range(JT)]
        eb = [sb.tile([P, 1], F32, name=f"eb{j}") for j in range(JT)]
        de = [sb.tile([P, 1], F32, name=f"de{j}") for j in range(JT)]
        res = [sb.tile([P, N], F32, name=f"res{j}") for j in range(JT)]
        for j in range(JT):
            nc.scalar.activation(out=sq[2 * j][:], in_=acc[0][j][:], func=ACT.Square, scale=root, accum_out=ea[j][:])
            nc.vector.tensor_tensor(b2[j][:], acc[1][j][:], bias[:], ALU.add)
        for j in range(JT):
            nc.scalar.activation(out=sq[2 * j + 1][:], in_=b2[j][:], func=ACT.Square, scale=root, accum_out=eb[j][:])
            nc.scalar.activation(out=de[j][:], in_=eb[j][:], func=ACT.Identity, scale=-1.0, bias=ea[j][:])
            nc.vector.tensor_tensor(gap[j][:], acc[0][j][:], b2[j][:], ALU.subtract)
        for j, queue in enumerate((nc.scalar, nc.sync)):
            nc.vector.tensor_scalar(res[j][:], gap[j][:], de[j][:], None, ALU.mult)
            queue.dma_start(out=out[j * P : (j + 1) * P, :], in_=res[j][:])
